import numpy as np
import ml_dtypes


def mxq(x, axis, fmt="e4m3"):
    dtype, down = {"e4m3": (ml_dtypes.float8_e4m3fn, 7), "e5m2": (ml_dtypes.float8_e5m2, 14)}[fmt]
    v = np.moveaxis(np.asarray(x, np.float32).astype(ml_dtypes.bfloat16).astype(np.float64), axis, -1)
    blocks = v.reshape(v.shape[:-1] + (-1, 32))
    amax = np.abs(blocks).max(-1, keepdims=True)
    byte = np.maximum(np.where(amax > 0, np.frexp(amax)[1] - 1 + 127, 0) - down, 1)
    scale = np.exp2(byte - 127.0)
    codes = (blocks / scale).astype(np.float32).astype(dtype).astype(np.float64)
    return np.moveaxis((codes * scale).reshape(v.shape), -1, axis)


WIDE = False


def mx_kscale(k):
    if not WIDE:
        return np.ones(k)
    levels = np.array([10, -10, 5, -5, 0])
    if k % 512:
        return np.exp2(np.random.permutation(np.resize(levels, k // 32))).repeat(32)
    a = np.empty((k // 512, 16))
    for p in range(k // 512):
        a[p, :8] = np.random.permutation(np.resize(levels, 8))
        for g in range(8):
            far = levels[np.abs(levels - a[p, g]) >= 10]
            a[p, g + 8] = far[np.random.randint(len(far))]
    return np.exp2(a.ravel()).repeat(32)


def f64(x):
    return np.asarray(x).astype(np.float64)


def striped(idx):
    return np.tile(idx.reshape(-1, 16).T, (8, 1)).astype(np.uint16)


def unstriped(offs):
    return offs[:16].T.reshape(-1).astype(np.int64)


def pack_weight(w):
    k, n = w.shape
    w = f64(np.asarray(w, np.float32).astype(ml_dtypes.bfloat16)).reshape(k // 32, 32, n)
    amax = np.abs(w).max(1)
    byte = np.clip(np.where(amax > 0, np.frexp(amax)[1] - 1 + 127 - 7, 1), 1, 254)
    scaled = (w * np.exp2(127.0 - byte)[:, None, :]).reshape(k, n).astype(np.float32)
    words = np.ascontiguousarray(scaled.reshape(k // 512, 128, 4, n).transpose(0, 1, 3, 2)).astype(ml_dtypes.float8_e4m3fn).view(np.uint8)
    return words, np.ascontiguousarray(byte.astype(np.uint8).reshape(k // 512, 16, n))


def unpack_weight(words, scales):
    g, p, n, _ = words.shape
    vals = np.ascontiguousarray(words).view(ml_dtypes.float8_e4m3fn).astype(np.float64) * np.repeat(np.exp2(scales.astype(np.float64) - 127.0), 8, axis=1)[..., None]
    return vals.transpose(0, 1, 3, 2).reshape(g * 512, n)


E2M1 = np.array([0.0, 0.5, 1.0, 1.5, 2.0, 3.0, 4.0, 6.0, -0.0, -0.5, -1.0, -1.5, -2.0, -3.0, -4.0, -6.0])


def pack_fp4(w):
    k, n = w.shape
    w = f64(np.asarray(w, np.float32).astype(ml_dtypes.bfloat16)).reshape(k // 32, 32, n)
    amax = np.abs(w).max(1)
    mant, ex = np.frexp(amax / 6.0)
    byte = np.clip(np.where(amax > 0, np.where(mant > 0.5, ex, ex - 1) + 127, 1), 1, 254)
    scaled = (w * np.exp2(127.0 - byte)[:, None, :]).reshape(k, n).astype(np.float32)
    c = np.ascontiguousarray(scaled.reshape(k // 512, 128, 4, n).transpose(0, 1, 3, 2)).astype(ml_dtypes.float4_e2m1fn).view(np.uint8) & 0xF
    words = (c[..., 0::2] | (c[..., 1::2] << 4)).reshape(k // 512, 128, 2 * n)
    return np.ascontiguousarray(words), np.ascontiguousarray(byte.astype(np.uint8).reshape(k // 512, 16, n))


def unpack_fp4(words, scales):
    g, _, n = scales.shape
    words = np.ascontiguousarray(words).reshape(g, 128, n, 2)
    nib = np.empty((g, 128, n, 4), np.uint8)
    nib[..., 0::2] = words & 0xF
    nib[..., 1::2] = words >> 4
    vals = E2M1[nib] * np.repeat(np.exp2(scales.astype(np.float64) - 127.0), 8, axis=1)[..., None]
    return vals.transpose(0, 1, 3, 2).reshape(g * 512, n)


def planes(y):
    n, m = y.shape
    v = y.astype(np.float32).astype(ml_dtypes.bfloat16).astype(np.float64).reshape(n // 32, 32, m)
    top = np.abs(v).max(1)
    byte = np.clip(np.where(top > 0, np.frexp(top)[1] - 1 + 127 - 7, 1), 1, 254)
    codes = (v * np.exp2(127.0 - byte)[:, None, :]).reshape(n, m).astype(np.float32).astype(ml_dtypes.float8_e4m3fn).view(np.uint8)
    words = codes.reshape(n // 512, 128, 4, m).transpose(0, 1, 3, 2)
    return np.ascontiguousarray(words), np.ascontiguousarray(byte.astype(np.uint8).reshape(n // 512, 16, m))


K, T, S, N, H, U = 1024, 2048, 512, 512, 512, 1024


def setup_inputs():
    n = np.random.standard_normal
    s = mx_kscale(K)[:, None]
    u = mx_kscale(H)
    packed_xT = pack_weight(n((K, T)) * s)
    packed_w1 = pack_fp4(n((K, N)) / np.sqrt(K) / s)
    packed_w2 = pack_fp4(n((K, N)) / np.sqrt(K) / s)
    packed_w3 = pack_fp4(n((H, N)) / np.sqrt(H) / u[:, None])
    return {
        "x_words": packed_xT[0],
        "x_scales": packed_xT[1],
        "w1_words": packed_w1[0],
        "w1_scales": packed_w1[1],
        "w2_words": packed_w2[0],
        "w2_scales": packed_w2[1],
        "unit": (np.random.uniform(0.6, 1.4, (H, 1)) * u[:, None]).astype(np.float32),
        "w3_words": packed_w3[0],
        "w3_scales": packed_w3[1],
        "offs": striped(np.random.permutation(T)[:S]),
        "u1": striped(np.random.permutation(np.concatenate([np.arange(S), np.random.randint(0, S, U - S)]))),
        "u2": striped(np.random.permutation(np.concatenate([np.arange(S), np.random.randint(0, S, U - S)]))),
    }


def reference(x_words, x_scales, w1_words, w1_scales, w2_words, w2_scales, unit, w3_words, w3_scales, offs, u1, u2):
    xq = unpack_weight(x_words, x_scales)[:, unstriped(offs)]
    y = unpack_fp4(w1_words, w1_scales).T @ xq
    y1 = y[:, unstriped(u1)]
    z1 = unpack_fp4(w2_words, w2_scales).T @ xq
    z2 = z1[:, unstriped(u2)]
    rep1 = y1 + z2
    y2 = y[:, unstriped(u2)]
    zu = z1[:, unstriped(u1)]
    hid = f64(unit) * (np.maximum(rep1, y2) * zu)
    out_0 = unpack_fp4(w3_words, w3_scales).T @ mxq(hid, 0, "e4m3")
    return (out_0,) + planes(out_0)

@@ -1,0 +1,221 @@
+from contextlib import ExitStack
+
+import concourse.mybir as mybir
+
+K, T, S, H, N, U = 1024, 2048, 512, 512, 512, 1024
+FLOPS = 2 * K * H * S * 2 + 2 * H * N * U
+
+F32 = mybir.dt.float32
+BF16 = mybir.dt.bfloat16
+I32 = mybir.dt.int32
+U32 = mybir.dt.uint32
+U16 = mybir.dt.uint16
+U8 = mybir.dt.uint8
+FP8X4 = mybir.dt.float8_e4m3fn_x4
+FP4X4 = mybir.dt.float4_e2m1fn_x4
+COPY = mybir.ActivationFunctionType.Copy
+ADD = mybir.AluOpType.add
+MULT = mybir.AluOpType.mult
+MAX = mybir.AluOpType.max
+
+P = 128
+PACK = 4
+PASSES = K // (P * PACK)
+SPARE = 16
+BANK = 512
+GROUP = BANK // PACK
+CHUNKS = (512, 256, 128, 128)
+
+
+def load_scale_rows(queue, plane, scales):
+    passes = scales.shape[0]
+    for q in range(4):
+        queue.dma_start(
+            out=plane[32 * q : 32 * q + 4, :].bitcast(I32).rearrange("p (o c) -> p o c", o=passes),
+            in_=scales[:, 4 * q : 4 * q + 4, :].bitcast(I32).rearrange("o q c -> q o c"),
+        )
+
+
+def deal_columns(nc, dealt, raw, passes):
+    nc.vector.tensor_copy(
+        out=dealt.rearrange("p (o t m) -> p o m t", o=passes, t=PACK),
+        in_=raw.rearrange("p (o m t) -> p o m t", o=passes, t=PACK),
+    )
+
+
+def tile_picked_ybackpt_max_po_kernel(
+    tc, x_words, x_scales, w1_words, w1_scales, w2_words, w2_scales, unit, w3_words, w3_scales,
+    offs, u1, u2, out_0, out_1, out_2,
+):
+    nc = tc.nc
+    with ExitStack() as ctx:
+        keep = ctx.enter_context(tc.tile_pool(name="keep", bufs=1))
+        ring = ctx.enter_context(tc.tile_pool(name="ring", bufs=3))
+        psum = ctx.enter_context(tc.psum_pool(name="psum", bufs=8))
+
+        offs_sb = keep.tile([P, S // 16], U16, name="offs_sb")
+        u1_sb = keep.tile([P, U // 16], U16, name="u1_sb")
+        u2_sb = keep.tile([P, U // 16], U16, name="u2_sb")
+
+        xs_all = keep.tile([P, PASSES * T], U8, name="xs_all", align_bytes=64)
+        nc.vector.memset(xs_all[:].bitcast(I32), 0)
+        weights = ((w1_words, w1_scales), (w2_words, w2_scales), (w3_words, w3_scales))
+        raw_words, raw_scales = [], []
+        for i, (words, scales) in enumerate(weights):
+            passes = words.shape[0]
+            raw_words.append(keep.tile([P, passes * 2 * H], U8, name=f"raw_words{i}", align_bytes=64))
+            raw_scales.append(keep.tile([P, passes * H], U8, name=f"raw_scales{i}", align_bytes=64))
+            nc.gpsimd.memset(raw_scales[i][:].bitcast(I32), 0)
+
+        def load_words(i):
+            words = weights[i][0]
+            nc.sync.dma_start(
+                out=raw_words[i][:].bitcast(I32).rearrange("p (o c) -> p o c", o=words.shape[0]),
+                in_=words.bitcast(I32).rearrange("o p c -> p o c"),
+            )
+
+        nc.sync.dma_start(offs_sb[:], offs)
+        load_scale_rows(nc.scalar, xs_all, x_scales)
+        load_words(0)
+        xw_all = []
+        for o in range(PASSES):
+            xw_all.append(keep.tile([P, T], U32, name=f"xw_all{o}", align_bytes=64))
+            nc.sync.dma_start(
+                out=xw_all[o][:].bitcast(I32),
+                in_=x_words[o].rearrange("p c r -> p (c r)").bitcast(I32),
+            )
+        load_scale_rows(nc.scalar, raw_scales[0], w1_scales)
+        load_words(1)
+        load_scale_rows(nc.scalar, raw_scales[1], w2_scales)
+        nc.sync.dma_start(u1_sb[:], u1)
+        nc.sync.dma_start(u2_sb[:], u2)
+        unit_sb = keep.tile([P, PACK], F32, name="unit_sb")
+        nc.sync.dma_start(out=unit_sb[:], in_=unit.rearrange("(p t) o -> p (t o)", t=PACK))
+        load_words(2)
+        load_scale_rows(nc.sync, raw_scales[2], w3_scales)
+
+        tables = {}
+        for kind in ("y", "z", "zu"):
+            for t in range(PACK):
+                tables[kind, t] = keep.tile([P, S + SPARE], F32, name=f"{kind}{t}")
+                nc.gpsimd.memset(tables[kind, t][:, S:], 0.0)
+
+        w_words, w_scales = [], []
+
+        def deal_weight(i):
+            passes = weights[i][0].shape[0]
+            w_words.append(keep.tile([P, passes * 2 * H], U8, name=f"w_words{i}", align_bytes=64))
+            w_scales.append(keep.tile([P, passes * H], U8, name=f"w_scales{i}", align_bytes=64))
+            deal_columns(nc, w_words[i][:].bitcast(U16), raw_words[i][:].bitcast(U16), passes)
+            deal_columns(nc, w_scales[i][:], raw_scales[i][:], passes)
+
+        xw, xs = [], []
+        for o in range(PASSES):
+            xs.append(keep.tile([P, S], U8, name=f"xs{o}", align_bytes=64))
+            nc.vector.tensor_copy(xs[o][:], xs_all[:, o * T : (o + 1) * T].indirect(offs_sb[:]))
+        deal_weight(0)
+        for o in range(PASSES):
+            xw.append(keep.tile([P, S], U32, name=f"xw{o}", align_bytes=64))
+            nc.vector.tensor_copy(xw[o][:], xw_all[o][:].indirect(offs_sb[:]))
+        deal_weight(1)
+        deal_weight(2)
+
+        def stationary(i, o, t):
+            c0 = o * H + t * P
+            return dict(
+                lhsT=w_words[i][:, 2 * c0 : 2 * (c0 + P)].bitcast(FP4X4),
+                lhsT_scale=w_scales[i][:, c0 : c0 + P],
+            )
+
+        def project(i, t):
+            acc = psum.tile([P, BANK], F32, name="acc")
+            for o in range(PASSES):
+                nc.tensor.matmul_mx(
+                    out=acc[:], rhs=xw[o][:].bitcast(FP8X4), rhs_scale=xs[o][:],
+                    start=(o == 0), stop=(o == PASSES - 1), **stationary(i, o, t),
+                )
+            return acc
+
+        def make_tables(t):
+            y_acc = project(0, t)
+            nc.scalar.copy(out=tables["y", t][:, :S], in_=y_acc[:])
+            z_acc = project(1, t)
+            if t < 2:
+                nc.vector.tensor_copy(out=tables["z", t][:, :S], in_=z_acc[:])
+                nc.vector.tensor_scalar(
+                    out=tables["zu", t][:, :S], in0=z_acc[:], scalar1=unit_sb[:, t : t + 1], scalar2=None, op0=MULT
+                )
+            else:
+                nc.scalar.copy(out=tables["z", t][:, :S], in_=z_acc[:])
+                nc.scalar.activation(tables["zu", t][:, :S], z_acc[:], COPY, scale=unit_sb[:, t : t + 1])
+
+        out_words = keep.tile([P, U], U32, name="out_words", align_bytes=64)
+        out_scales = keep.tile([P, U], U8, name="out_scales", align_bytes=64)
+        out_rows = out_0.rearrange("(p t) r -> p t r", t=PACK)
+        out_words_hbm = out_1[0].rearrange("p c r -> p (c r)").bitcast(I32)
+
+        r0 = 0
+        for ci, n in enumerate(CHUNKS):
+            last = ci == len(CHUNKS) - 1
+            lists = slice(r0 // 16, (r0 + n) // 16)
+            hid = keep.tile([P, PACK, n], F32, name=f"hid{ci}")
+            per_step = BANK // n
+            for t0 in range(0, PACK, per_step):
+                if ci == 0:
+                    make_tables(t0)
+                y1 = ring.tile([P, per_step, n], F32, name="y1")
+                y2 = ring.tile([P, per_step, n], F32, name="y2")
+                rep = ring.tile([P, per_step, n], F32, name="rep")
+                top = ring.tile([P, per_step, n], F32, name="top")
+                for j in range(per_step):
+                    nc.scalar.activation(y1[:, j, :], tables["y", t0 + j][:].indirect(u1_sb[:, lists]), COPY)
+                for j in range(per_step):
+                    nc.scalar.activation(y2[:, j, :], tables["y", t0 + j][:].indirect(u2_sb[:, lists]), COPY)
+                for j in range(per_step):
+                    nc.vector.tensor_tensor(rep[:, j, :], tables["z", t0 + j][:].indirect(u2_sb[:, lists]), y1[:, j, :], ADD)
+                nc.vector.tensor_tensor(top[:], rep[:], y2[:], MAX)
+                for j in range(per_step):
+                    nc.vector.tensor_tensor(
+                        hid[:, t0 + j, :], tables["zu", t0 + j][:].indirect(u1_sb[:, lists]), top[:, j, :], MULT
+                    )
+            hid_bf = keep.tile([P, n, PACK], BF16, name=f"hid_bf{ci}", align_bytes=64)
+            nc.vector.tensor_copy(
+                out=hid_bf[:].rearrange("p (c i) t -> p c t i", i=4),
+                in_=hid[:].rearrange("p t (c i) -> p c t i", i=4),
+            )
+            hid_words = keep.tile([P, n], U32, name=f"hid_words{ci}", align_bytes=64)
+            hid_scales = keep.tile([P, n], U8, name=f"hid_scales{ci}", align_bytes=64)
+            nc.vector.quantize_mx(
+                out=hid_words[:].bitcast(FP8X4), scales=hid_scales[:], in_=hid_bf[:].rearrange("p c t -> p (c t)")
+            )
+            res = keep.tile([P, PACK, n], F32, name=f"res{ci}")
+            res_bf = keep.tile([P, n, PACK], BF16, name=f"res_bf{ci}", align_bytes=64)
+            for g0 in range(0, n, GROUP):
+                cols = slice(g0, g0 + GROUP)
+                acc = psum.tile([P, PACK, GROUP], F32, name="acc")
+                for t in range(PACK):
+                    nc.tensor.matmul_mx(
+                        out=acc[:, t, :], rhs=hid_words[:, cols].bitcast(FP8X4), rhs_scale=hid_scales[:, cols],
+                        start=True, stop=True, **stationary(2, 0, t),
+                    )
+                if last:
+                    nc.vector.tensor_copy(out=res_bf[:, cols, :], in_=acc[:].rearrange("p t c -> p c t"))
+                else:
+                    nc.scalar.copy(out=res_bf[:, cols, :], in_=acc[:].rearrange("p t c -> p c t"))
+                nc.scalar.copy(out=res[:, :, cols], in_=acc[:])
+            done = slice(r0, r0 + n)
+            nc.vector.quantize_mx(
+                out=out_words[:, done].bitcast(FP8X4), scales=out_scales[:, done],
+                in_=res_bf[:].rearrange("p c t -> p (c t)"),
+            )
+            nc.sync.dma_start(out=out_rows[:, :, done], in_=res[:])
+            nc.sync.dma_start(out=out_words_hbm[:, done], in_=out_words[:, done].bitcast(I32))
+            if ci >= len(CHUNKS) - 2:
+                span = done if last else slice(0, r0 + n)
+                for q in range(4):
+                    queue = nc.scalar if last and q % 2 else nc.sync
+                    queue.dma_start(
+                        out=out_2[0, 4 * q : 4 * q + 4, span].bitcast(I32),
+                        in_=out_scales[32 * q : 32 * q + 4, span].bitcast(I32),
+                    )
+            r0 = r0 + n

@@ -24,7 +24,7 @@ PASSES = K // (P * PACK)
 SPARE = 16
 BANK = 512
 GROUP = BANK // PACK
-CHUNKS = (512, 256, 128, 128)
+CHUNKS = (512, 384, 128)
 
 
 def load_scale_rows(queue, plane, scales):
@@ -50,7 +50,7 @@ def tile_picked_ybackpt_max_po_kernel(
     nc = tc.nc
     with ExitStack() as ctx:
         keep = ctx.enter_context(tc.tile_pool(name="keep", bufs=1))
-        ring = ctx.enter_context(tc.tile_pool(name="ring", bufs=3))
+        ring = ctx.enter_context(tc.tile_pool(name="ring", bufs=4))
         psum = ctx.enter_context(tc.psum_pool(name="psum", bufs=8))
 
         offs_sb = keep.tile([P, S // 16], U16, name="offs_sb")
@@ -58,14 +58,16 @@ def tile_picked_ybackpt_max_po_kernel(
         u2_sb = keep.tile([P, U // 16], U16, name="u2_sb")
 
         xs_all = keep.tile([P, PASSES * T], U8, name="xs_all", align_bytes=64)
-        nc.vector.memset(xs_all[:].bitcast(I32), 0)
+        nc.gpsimd.memset(xs_all[:, :T].bitcast(I32), 0)
+        nc.vector.memset(xs_all[:, T:].bitcast(I32), 0)
         weights = ((w1_words, w1_scales), (w2_words, w2_scales), (w3_words, w3_scales))
         raw_words, raw_scales = [], []
         for i, (words, scales) in enumerate(weights):
             passes = words.shape[0]
             raw_words.append(keep.tile([P, passes * 2 * H], U8, name=f"raw_words{i}", align_bytes=64))
             raw_scales.append(keep.tile([P, passes * H], U8, name=f"raw_scales{i}", align_bytes=64))
-            nc.gpsimd.memset(raw_scales[i][:].bitcast(I32), 0)
+            clearer = nc.vector if i == 0 else nc.gpsimd
+            clearer.memset(raw_scales[i][:].bitcast(I32), 0)
 
         def load_words(i):
             words = weights[i][0]
@@ -74,20 +76,23 @@ def tile_picked_ybackpt_max_po_kernel(
                 in_=words.bitcast(I32).rearrange("o p c -> p o c"),
             )
 
-        nc.sync.dma_start(offs_sb[:], offs)
-        load_scale_rows(nc.scalar, xs_all, x_scales)
-        load_words(0)
-        xw_all = []
-        for o in range(PASSES):
-            xw_all.append(keep.tile([P, T], U32, name=f"xw_all{o}", align_bytes=64))
+        xw_all = [keep.tile([P, T], U32, name=f"xw_all{o}", align_bytes=64) for o in range(PASSES)]
+
+        def load_x_words(o):
             nc.sync.dma_start(
                 out=xw_all[o][:].bitcast(I32),
                 in_=x_words[o].rearrange("p c r -> p (c r)").bitcast(I32),
             )
-        load_scale_rows(nc.scalar, raw_scales[0], w1_scales)
-        load_words(1)
-        load_scale_rows(nc.scalar, raw_scales[1], w2_scales)
+
+        nc.sync.dma_start(offs_sb[:], offs)
+        load_words(0)
         nc.sync.dma_start(u1_sb[:], u1)
+        load_scale_rows(nc.sync, xs_all, x_scales)
+        load_x_words(0)
+        load_scale_rows(nc.sync, raw_scales[0], w1_scales)
+        load_x_words(1)
+        load_scale_rows(nc.sync, raw_scales[1], w2_scales)
+        load_words(1)
         nc.sync.dma_start(u2_sb[:], u2)
         unit_sb = keep.tile([P, PACK], F32, name="unit_sb")
         nc.sync.dma_start(out=unit_sb[:], in_=unit.rearrange("(p t) o -> p (t o)", t=PACK))
@@ -110,10 +115,10 @@ def tile_picked_ybackpt_max_po_kernel(
             deal_columns(nc, w_scales[i][:], raw_scales[i][:], passes)
 
         xw, xs = [], []
+        deal_weight(0)
         for o in range(PASSES):
             xs.append(keep.tile([P, S], U8, name=f"xs{o}", align_bytes=64))
             nc.vector.tensor_copy(xs[o][:], xs_all[:, o * T : (o + 1) * T].indirect(offs_sb[:]))
-        deal_weight(0)
         for o in range(PASSES):
             xw.append(keep.tile([P, S], U32, name=f"xw{o}", align_bytes=64))
             nc.vector.tensor_copy(xw[o][:], xw_all[o][:].indirect(offs_sb[:]))
@@ -142,21 +147,23 @@ def tile_picked_ybackpt_max_po_kernel(
             z_acc = project(1, t)
             if t < 2:
                 nc.vector.tensor_copy(out=tables["z", t][:, :S], in_=z_acc[:])
-                nc.vector.tensor_scalar(
-                    out=tables["zu", t][:, :S], in0=z_acc[:], scalar1=unit_sb[:, t : t + 1], scalar2=None, op0=MULT
-                )
             else:
                 nc.scalar.copy(out=tables["z", t][:, :S], in_=z_acc[:])
-                nc.scalar.activation(tables["zu", t][:, :S], z_acc[:], COPY, scale=unit_sb[:, t : t + 1])
+            nc.vector.tensor_scalar(
+                out=tables["zu", t][:, :S], in0=tables["z", t][:, :S], scalar1=unit_sb[:, t : t + 1],
+                scalar2=None, op0=MULT,
+            )
 
         out_words = keep.tile([P, U], U32, name="out_words", align_bytes=64)
         out_scales = keep.tile([P, U], U8, name="out_scales", align_bytes=64)
         out_rows = out_0.rearrange("(p t) r -> p t r", t=PACK)
         out_words_hbm = out_1[0].rearrange("p c r -> p (c r)").bitcast(I32)
 
-        r0 = 0
-        for ci, n in enumerate(CHUNKS):
-            last = ci == len(CHUNKS) - 1
+        starts = [sum(CHUNKS[:ci]) for ci in range(len(CHUNKS))]
+        final = len(CHUNKS) - 1
+
+        def hidden(ci):
+            n, r0 = CHUNKS[ci], starts[ci]
             lists = slice(r0 // 16, (r0 + n) // 16)
             hid = keep.tile([P, PACK, n], F32, name=f"hid{ci}")
             per_step = BANK // n
@@ -188,8 +195,7 @@ def tile_picked_ybackpt_max_po_kernel(
             nc.vector.quantize_mx(
                 out=hid_words[:].bitcast(FP8X4), scales=hid_scales[:], in_=hid_bf[:].rearrange("p c t -> p (c t)")
             )
-            res = keep.tile([P, PACK, n], F32, name=f"res{ci}")
-            res_bf = keep.tile([P, n, PACK], BF16, name=f"res_bf{ci}", align_bytes=64)
+            banks = []
             for g0 in range(0, n, GROUP):
                 cols = slice(g0, g0 + GROUP)
                 acc = psum.tile([P, PACK, GROUP], F32, name="acc")
@@ -198,24 +204,45 @@ def tile_picked_ybackpt_max_po_kernel(
                         out=acc[:, t, :], rhs=hid_words[:, cols].bitcast(FP8X4), rhs_scale=hid_scales[:, cols],
                         start=True, stop=True, **stationary(2, 0, t),
                     )
-                if last:
+                banks.append((cols, acc))
+            return banks
+
+        def store_values(ci, banks):
+            n, r0 = CHUNKS[ci], starts[ci]
+            res = keep.tile([P, PACK, n], F32, name=f"res{ci}")
+            for cols, acc in banks:
+                nc.scalar.copy(out=res[:, :, cols], in_=acc[:])
+            nc.sync.dma_start(out=out_rows[:, :, r0 : r0 + n], in_=res[:])
+
+        def store_planes(ci, banks):
+            n, r0 = CHUNKS[ci], starts[ci]
+            done = slice(r0, r0 + n)
+            res_bf = keep.tile([P, n, PACK], BF16, name=f"res_bf{ci}", align_bytes=64)
+            for cols, acc in banks:
+                if ci == final:
                     nc.vector.tensor_copy(out=res_bf[:, cols, :], in_=acc[:].rearrange("p t c -> p c t"))
                 else:
                     nc.scalar.copy(out=res_bf[:, cols, :], in_=acc[:].rearrange("p t c -> p c t"))
-                nc.scalar.copy(out=res[:, :, cols], in_=acc[:])
-            done = slice(r0, r0 + n)
             nc.vector.quantize_mx(
                 out=out_words[:, done].bitcast(FP8X4), scales=out_scales[:, done],
                 in_=res_bf[:].rearrange("p c t -> p (c t)"),
             )
-            nc.sync.dma_start(out=out_rows[:, :, done], in_=res[:])
             nc.sync.dma_start(out=out_words_hbm[:, done], in_=out_words[:, done].bitcast(I32))
-            if ci >= len(CHUNKS) - 2:
-                span = done if last else slice(0, r0 + n)
+            if ci >= final - 1:
+                span = done if ci == final else slice(0, r0 + n)
                 for q in range(4):
-                    queue = nc.scalar if last and q % 2 else nc.sync
+                    queue = nc.scalar if ci == final and q % 2 else nc.sync
                     queue.dma_start(
                         out=out_2[0, 4 * q : 4 * q + 4, span].bitcast(I32),
                         in_=out_scales[32 * q : 32 * q + 4, span].bitcast(I32),
                     )
-            r0 = r0 + n
+
+        before = None
+        for ci in range(len(CHUNKS)):
+            banks = hidden(ci)
+            if before is not None:
+                store_planes(ci - 1, before)
+            if ci == final:
+                store_planes(ci, banks)
+            store_values(ci, banks)
+            before = banks

@@ -25,6 +25,7 @@ SPARE = 16
 BANK = 512
 GROUP = BANK // PACK
 CHUNKS = (512, 384, 128)
+STEP_COLUMNS = 256
 
 
 def load_scale_rows(queue, plane, scales):
@@ -38,8 +39,8 @@ def load_scale_rows(queue, plane, scales):
 
 def deal_columns(nc, dealt, raw, passes):
     nc.vector.tensor_copy(
-        out=dealt.rearrange("p (o t m) -> p o m t", o=passes, t=PACK),
-        in_=raw.rearrange("p (o m t) -> p o m t", o=passes, t=PACK),
+        out=dealt.rearrange("p (o t m) -> p o t m", o=passes, t=PACK),
+        in_=raw.rearrange("p (o m t) -> p o t m", o=passes, t=PACK),
     )
 
 
@@ -161,35 +162,50 @@ def tile_picked_ybackpt_max_po_kernel(
 
         starts = [sum(CHUNKS[:ci]) for ci in range(len(CHUNKS))]
         final = len(CHUNKS) - 1
+        hid = [keep.tile([P, PACK, n], F32, name=f"hid{ci}") for ci, n in enumerate(CHUNKS)]
+        steps = []
+        for ci, n in enumerate(CHUNKS):
+            tiles_a_step = max(1, STEP_COLUMNS // n)
+            steps.extend((ci, range(t0, t0 + tiles_a_step)) for t0 in range(0, PACK, tiles_a_step))
 
-        def hidden(ci):
-            n, r0 = CHUNKS[ci], starts[ci]
-            lists = slice(r0 // 16, (r0 + n) // 16)
-            hid = keep.tile([P, PACK, n], F32, name=f"hid{ci}")
-            per_step = BANK // n
-            for t0 in range(0, PACK, per_step):
-                if ci == 0:
-                    make_tables(t0)
-                y1 = ring.tile([P, per_step, n], F32, name="y1")
-                y2 = ring.tile([P, per_step, n], F32, name="y2")
-                rep = ring.tile([P, per_step, n], F32, name="rep")
-                top = ring.tile([P, per_step, n], F32, name="top")
-                for j in range(per_step):
-                    nc.scalar.activation(y1[:, j, :], tables["y", t0 + j][:].indirect(u1_sb[:, lists]), COPY)
-                for j in range(per_step):
-                    nc.scalar.activation(y2[:, j, :], tables["y", t0 + j][:].indirect(u2_sb[:, lists]), COPY)
-                for j in range(per_step):
-                    nc.vector.tensor_tensor(rep[:, j, :], tables["z", t0 + j][:].indirect(u2_sb[:, lists]), y1[:, j, :], ADD)
-                nc.vector.tensor_tensor(top[:], rep[:], y2[:], MAX)
-                for j in range(per_step):
-                    nc.vector.tensor_tensor(
-                        hid[:, t0 + j, :], tables["zu", t0 + j][:].indirect(u1_sb[:, lists]), top[:, j, :], MULT
-                    )
-            hid_bf = keep.tile([P, n, PACK], BF16, name=f"hid_bf{ci}", align_bytes=64)
-            nc.vector.tensor_copy(
+        def entries(ci):
+            return slice(starts[ci] // 16, (starts[ci] + CHUNKS[ci]) // 16)
+
+        def fetch_and_add(ci, ts):
+            shape = [P, len(ts), CHUNKS[ci]]
+            y1 = ring.tile(shape, F32, name="y1")
+            y2 = ring.tile(shape, F32, name="y2")
+            rep = ring.tile(shape, F32, name="rep")
+            for j, t in enumerate(ts):
+                nc.scalar.activation(y1[:, j, :], tables["y", t][:].indirect(u1_sb[:, entries(ci)]), COPY)
+            for j, t in enumerate(ts):
+                nc.scalar.activation(y2[:, j, :], tables["y", t][:].indirect(u2_sb[:, entries(ci)]), COPY)
+            for j, t in enumerate(ts):
+                nc.vector.tensor_tensor(rep[:, j, :], tables["z", t][:].indirect(u2_sb[:, entries(ci)]), y1[:, j, :], ADD)
+            return rep, y2
+
+        def larger(ci, ts, rep, y2):
+            top = ring.tile([P, len(ts), CHUNKS[ci]], F32, name="top")
+            nc.vector.tensor_tensor(top[:], rep[:], y2[:], MAX)
+            return top
+
+        def fetch_and_multiply(ci, ts, top):
+            for j, t in enumerate(ts):
+                nc.vector.tensor_tensor(
+                    hid[ci][:, t, :], tables["zu", t][:].indirect(u1_sb[:, entries(ci)]), top[:, j, :], MULT
+                )
+
+        def round_hidden(ci):
+            hid_bf = keep.tile([P, CHUNKS[ci], PACK], BF16, name=f"hid_bf{ci}", align_bytes=64)
+            rounding_copy = nc.scalar.copy if ci == 0 else nc.vector.tensor_copy
+            rounding_copy(
                 out=hid_bf[:].rearrange("p (c i) t -> p c t i", i=4),
-                in_=hid[:].rearrange("p t (c i) -> p c t i", i=4),
+                in_=hid[ci][:].rearrange("p t (c i) -> p c t i", i=4),
             )
+            return hid_bf
+
+        def last_product(ci, hid_bf):
+            n = CHUNKS[ci]
             hid_words = keep.tile([P, n], U32, name=f"hid_words{ci}", align_bytes=64)
             hid_scales = keep.tile([P, n], U8, name=f"hid_scales{ci}", align_bytes=64)
             nc.vector.quantize_mx(
@@ -214,35 +230,50 @@ def tile_picked_ybackpt_max_po_kernel(
                 nc.scalar.copy(out=res[:, :, cols], in_=acc[:])
             nc.sync.dma_start(out=out_rows[:, :, r0 : r0 + n], in_=res[:])
 
-        def store_planes(ci, banks):
-            n, r0 = CHUNKS[ci], starts[ci]
-            done = slice(r0, r0 + n)
-            res_bf = keep.tile([P, n, PACK], BF16, name=f"res_bf{ci}", align_bytes=64)
+        def round_values(ci, banks):
+            res_bf = keep.tile([P, CHUNKS[ci], PACK], BF16, name=f"res_bf{ci}", align_bytes=64)
             for cols, acc in banks:
                 if ci == final:
                     nc.vector.tensor_copy(out=res_bf[:, cols, :], in_=acc[:].rearrange("p t c -> p c t"))
                 else:
                     nc.scalar.copy(out=res_bf[:, cols, :], in_=acc[:].rearrange("p t c -> p c t"))
+            return res_bf
+
+        def store_words(ci, res_bf):
+            done = slice(starts[ci], starts[ci] + CHUNKS[ci])
             nc.vector.quantize_mx(
                 out=out_words[:, done].bitcast(FP8X4), scales=out_scales[:, done],
                 in_=res_bf[:].rearrange("p c t -> p (c t)"),
             )
             nc.sync.dma_start(out=out_words_hbm[:, done], in_=out_words[:, done].bitcast(I32))
-            if ci >= final - 1:
-                span = done if ci == final else slice(0, r0 + n)
-                for q in range(4):
-                    queue = nc.scalar if ci == final and q % 2 else nc.sync
-                    queue.dma_start(
-                        out=out_2[0, 4 * q : 4 * q + 4, span].bitcast(I32),
-                        in_=out_scales[32 * q : 32 * q + 4, span].bitcast(I32),
-                    )
 
-        before = None
-        for ci in range(len(CHUNKS)):
-            banks = hidden(ci)
-            if before is not None:
-                store_planes(ci - 1, before)
-            if ci == final:
-                store_planes(ci, banks)
-            store_values(ci, banks)
-            before = banks
+        waiting_top = None
+        waiting_hidden = None
+        waiting_values = None
+        for ci, ts in steps:
+            if ci == 0:
+                make_tables(ts[0])
+            rep, y2 = fetch_and_add(ci, ts)
+            if waiting_hidden is not None:
+                banks = last_product(*waiting_hidden)
+                store_values(waiting_hidden[0], banks)
+                if waiting_values is not None:
+                    store_words(*waiting_values)
+                waiting_values = (waiting_hidden[0], round_values(waiting_hidden[0], banks))
+                waiting_hidden = None
+            if waiting_top is not None:
+                fetch_and_multiply(*waiting_top)
+            top = larger(ci, ts, rep, y2)
+            if waiting_top is not None and waiting_top[0] != ci:
+                waiting_hidden = (waiting_top[0], round_hidden(waiting_top[0]))
+            waiting_top = (ci, ts, top)
+        fetch_and_multiply(*waiting_top)
+        banks = last_product(final, round_hidden(final))
+        store_words(*waiting_values)
+        store_words(final, round_values(final, banks))
+        store_values(final, banks)
+        for q in range(4):
+            queue = nc.scalar if q % 2 else nc.sync
+            queue.dma_start(
+                out=out_2[0, 4 * q : 4 * q + 4, :].bitcast(I32), in_=out_scales[32 * q : 32 * q + 4, :].bitcast(I32)
+            )

@@ -51,7 +51,7 @@ def tile_picked_ybackpt_max_po_kernel(
     nc = tc.nc
     with ExitStack() as ctx:
         keep = ctx.enter_context(tc.tile_pool(name="keep", bufs=1))
-        ring = ctx.enter_context(tc.tile_pool(name="ring", bufs=4))
+        ring = ctx.enter_context(tc.tile_pool(name="ring", bufs=3))
         psum = ctx.enter_context(tc.psum_pool(name="psum", bufs=8))
 
         offs_sb = keep.tile([P, S // 16], U16, name="offs_sb")
@@ -122,7 +122,11 @@ def tile_picked_ybackpt_max_po_kernel(
             nc.vector.tensor_copy(xs[o][:], xs_all[:, o * T : (o + 1) * T].indirect(offs_sb[:]))
         for o in range(PASSES):
             xw.append(keep.tile([P, S], U32, name=f"xw{o}", align_bytes=64))
-            nc.vector.tensor_copy(xw[o][:], xw_all[o][:].indirect(offs_sb[:]))
+            pieces = 2 if o == PASSES - 1 else 1
+            for h in range(pieces):
+                picked = slice(h * S // pieces, (h + 1) * S // pieces)
+                listed = slice(picked.start // 16, picked.stop // 16)
+                nc.vector.tensor_copy(xw[o][:, picked], xw_all[o][:].indirect(offs_sb[:, listed]))
         deal_weight(1)
         deal_weight(2)
 
@@ -136,17 +140,20 @@ def tile_picked_ybackpt_max_po_kernel(
         def project(i, t):
             acc = psum.tile([P, BANK], F32, name="acc")
             for o in range(PASSES):
-                nc.tensor.matmul_mx(
-                    out=acc[:], rhs=xw[o][:].bitcast(FP8X4), rhs_scale=xs[o][:],
-                    start=(o == 0), stop=(o == PASSES - 1), **stationary(i, o, t),
-                )
+                pieces = 2 if o == PASSES - 1 and (i, t) == (0, 0) else 1
+                for h in range(pieces):
+                    picked = slice(h * S // pieces, (h + 1) * S // pieces)
+                    nc.tensor.matmul_mx(
+                        out=acc[:, picked], rhs=xw[o][:, picked].bitcast(FP8X4), rhs_scale=xs[o][:, picked],
+                        start=(o == 0), stop=(o == PASSES - 1 and h == pieces - 1), **stationary(i, o, t),
+                    )
             return acc
 
         def make_tables(t):
             y_acc = project(0, t)
             nc.scalar.copy(out=tables["y", t][:, :S], in_=y_acc[:])
             z_acc = project(1, t)
-            if t < 2:
+            if t < 3:
                 nc.vector.tensor_copy(out=tables["z", t][:, :S], in_=z_acc[:])
             else:
                 nc.scalar.copy(out=tables["z", t][:, :S], in_=z_acc[:])
@@ -267,6 +274,11 @@ def tile_picked_ybackpt_max_po_kernel(
             if waiting_top is not None and waiting_top[0] != ci:
                 waiting_hidden = (waiting_top[0], round_hidden(waiting_top[0]))
             waiting_top = (ci, ts, top)
+        if waiting_hidden is not None:
+            banks = last_product(*waiting_hidden)
+            store_values(waiting_hidden[0], banks)
+            store_words(*waiting_values)
+            waiting_values = (waiting_hidden[0], round_values(waiting_hidden[0], banks))
         fetch_and_multiply(*waiting_top)
         banks = last_product(final, round_hidden(final))
         store_words(*waiting_values)

from contextlib import ExitStack

import concourse.mybir as mybir

K, T, S, H, N, U = 1024, 2048, 512, 512, 512, 1024
FLOPS = 2 * K * H * S * 2 + 2 * H * N * U

F32 = mybir.dt.float32
BF16 = mybir.dt.bfloat16
I32 = mybir.dt.int32
U32 = mybir.dt.uint32
U16 = mybir.dt.uint16
U8 = mybir.dt.uint8
FP8X4 = mybir.dt.float8_e4m3fn_x4
FP4X4 = mybir.dt.float4_e2m1fn_x4
COPY = mybir.ActivationFunctionType.Copy
ADD = mybir.AluOpType.add
MULT = mybir.AluOpType.mult
MAX = mybir.AluOpType.max

P = 128
PACK = 4
PASSES = K // (P * PACK)
SPARE = 16
BANK = 512
GROUP = BANK // PACK
CHUNKS = (512, 384, 128)
STEP_COLUMNS = 256


def load_scale_rows(queue, plane, scales):
    passes = scales.shape[0]
    for q in range(4):
        queue.dma_start(
            out=plane[32 * q : 32 * q + 4, :].bitcast(I32).rearrange("p (o c) -> p o c", o=passes),
            in_=scales[:, 4 * q : 4 * q + 4, :].bitcast(I32).rearrange("o q c -> q o c"),
        )


def deal_columns(nc, dealt, raw, passes):
    nc.vector.tensor_copy(
        out=dealt.rearrange("p (o t m) -> p o t m", o=passes, t=PACK),
        in_=raw.rearrange("p (o m t) -> p o t m", o=passes, t=PACK),
    )


def tile_picked_ybackpt_max_po_kernel(
    tc, x_words, x_scales, w1_words, w1_scales, w2_words, w2_scales, unit, w3_words, w3_scales,
    offs, u1, u2, out_0, out_1, out_2,
):
    nc = tc.nc
    with ExitStack() as ctx:
        keep = ctx.enter_context(tc.tile_pool(name="keep", bufs=1))
        ring = ctx.enter_context(tc.tile_pool(name="ring", bufs=3))
        psum = ctx.enter_context(tc.psum_pool(name="psum", bufs=8))

        offs_sb = keep.tile([P, S // 16], U16, name="offs_sb")
        u1_sb = keep.tile([P, U // 16], U16, name="u1_sb")
        u2_sb = keep.tile([P, U // 16], U16, name="u2_sb")

        xs_all = keep.tile([P, PASSES * T], U8, name="xs_all", align_bytes=64)
        nc.gpsimd.memset(xs_all[:, :T].bitcast(I32), 0)
        nc.vector.memset(xs_all[:, T:].bitcast(I32), 0)
        weights = ((w1_words, w1_scales), (w2_words, w2_scales), (w3_words, w3_scales))
        raw_words, raw_scales = [], []
        for i, (words, scales) in enumerate(weights):
            passes = words.shape[0]
            raw_words.append(keep.tile([P, passes * 2 * H], U8, name=f"raw_words{i}", align_bytes=64))
            raw_scales.append(keep.tile([P, passes * H], U8, name=f"raw_scales{i}", align_bytes=64))
            clearer = nc.vector if i == 0 else nc.gpsimd
            clearer.memset(raw_scales[i][:].bitcast(I32), 0)

        def load_words(i):
            words = weights[i][0]
            nc.sync.dma_start(
                out=raw_words[i][:].bitcast(I32).rearrange("p (o c) -> p o c", o=words.shape[0]),
                in_=words.bitcast(I32).rearrange("o p c -> p o c"),
            )

        xw_all = [keep.tile([P, T], U32, name=f"xw_all{o}", align_bytes=64) for o in range(PASSES)]

        def load_x_words(o):
            nc.sync.dma_start(
                out=xw_all[o][:].bitcast(I32),
                in_=x_words[o].rearrange("p c r -> p (c r)").bitcast(I32),
            )

        nc.sync.dma_start(offs_sb[:], offs)
        load_words(0)
        nc.sync.dma_start(u1_sb[:], u1)
        load_scale_rows(nc.sync, xs_all, x_scales)
        load_x_words(0)
        load_scale_rows(nc.sync, raw_scales[0], w1_scales)
        load_x_words(1)
        load_scale_rows(nc.sync, raw_scales[1], w2_scales)
        load_words(1)
        nc.sync.dma_start(u2_sb[:], u2)
        unit_sb = keep.tile([P, PACK], F32, name="unit_sb")
        nc.sync.dma_start(out=unit_sb[:], in_=unit.rearrange("(p t) o -> p (t o)", t=PACK))
        load_words(2)
        load_scale_rows(nc.sync, raw_scales[2], w3_scales)

        tables = {}
        for kind in ("y", "z", "zu"):
            for t in range(PACK):
                tables[kind, t] = keep.tile([P, S + SPARE], F32, name=f"{kind}{t}")
                nc.gpsimd.memset(tables[kind, t][:, S:], 0.0)

        w_words, w_scales = [], []

        def deal_weight(i):
            passes = weights[i][0].shape[0]
            w_words.append(keep.tile([P, passes * 2 * H], U8, name=f"w_words{i}", align_bytes=64))
            w_scales.append(keep.tile([P, passes * H], U8, name=f"w_scales{i}", align_bytes=64))
            deal_columns(nc, w_words[i][:].bitcast(U16), raw_words[i][:].bitcast(U16), passes)
            deal_columns(nc, w_scales[i][:], raw_scales[i][:], passes)

        xw, xs = [], []
        deal_weight(0)
        for o in range(PASSES):
            xs.append(keep.tile([P, S], U8, name=f"xs{o}", align_bytes=64))
            nc.vector.tensor_copy(xs[o][:], xs_all[:, o * T : (o + 1) * T].indirect(offs_sb[:]))
        for o in range(PASSES):
            xw.append(keep.tile([P, S], U32, name=f"xw{o}", align_bytes=64))
            pieces = 2 if o == PASSES - 1 else 1
            for h in range(pieces):
                picked = slice(h * S // pieces, (h + 1) * S // pieces)
                listed = slice(picked.start // 16, picked.stop // 16)
                nc.vector.tensor_copy(xw[o][:, picked], xw_all[o][:].indirect(offs_sb[:, listed]))
        deal_weight(1)
        deal_weight(2)

        def stationary(i, o, t):
            c0 = o * H + t * P
            return dict(
                lhsT=w_words[i][:, 2 * c0 : 2 * (c0 + P)].bitcast(FP4X4),
                lhsT_scale=w_scales[i][:, c0 : c0 + P],
            )

        def project(i, t):
            acc = psum.tile([P, BANK], F32, name="acc")
            for o in range(PASSES):
                pieces = 2 if o == PASSES - 1 and (i, t) == (0, 0) else 1
                for h in range(pieces):
                    picked = slice(h * S // pieces, (h + 1) * S // pieces)
                    nc.tensor.matmul_mx(
                        out=acc[:, picked], rhs=xw[o][:, picked].bitcast(FP8X4), rhs_scale=xs[o][:, picked],
                        start=(o == 0), stop=(o == PASSES - 1 and h == pieces - 1), **stationary(i, o, t),
                    )
            return acc

        def make_tables(t):
            y_acc = project(0, t)
            nc.scalar.copy(out=tables["y", t][:, :S], in_=y_acc[:])
            z_acc = project(1, t)
            if t < 3:
                nc.vector.tensor_copy(out=tables["z", t][:, :S], in_=z_acc[:])
            else:
                nc.scalar.copy(out=tables["z", t][:, :S], in_=z_acc[:])
            nc.vector.tensor_scalar(
                out=tables["zu", t][:, :S], in0=tables["z", t][:, :S], scalar1=unit_sb[:, t : t + 1],
                scalar2=None, op0=MULT,
            )

        out_words = keep.tile([P, U], U32, name="out_words", align_bytes=64)
        out_scales = keep.tile([P, U], U8, name="out_scales", align_bytes=64)
        out_rows = out_0.rearrange("(p t) r -> p t r", t=PACK)
        out_words_hbm = out_1[0].rearrange("p c r -> p (c r)").bitcast(I32)

        starts = [sum(CHUNKS[:ci]) for ci in range(len(CHUNKS))]
        final = len(CHUNKS) - 1
        hid = [keep.tile([P, PACK, n], F32, name=f"hid{ci}") for ci, n in enumerate(CHUNKS)]
        steps = []
        for ci, n in enumerate(CHUNKS):
            tiles_a_step = max(1, STEP_COLUMNS // n)
            steps.extend((ci, range(t0, t0 + tiles_a_step)) for t0 in range(0, PACK, tiles_a_step))

        def entries(ci):
            return slice(starts[ci] // 16, (starts[ci] + CHUNKS[ci]) // 16)

        def fetch_and_add(ci, ts):
            shape = [P, len(ts), CHUNKS[ci]]
            y1 = ring.tile(shape, F32, name="y1")
            y2 = ring.tile(shape, F32, name="y2")
            rep = ring.tile(shape, F32, name="rep")
            for j, t in enumerate(ts):
                nc.scalar.activation(y1[:, j, :], tables["y", t][:].indirect(u1_sb[:, entries(ci)]), COPY)
            for j, t in enumerate(ts):
                nc.scalar.activation(y2[:, j, :], tables["y", t][:].indirect(u2_sb[:, entries(ci)]), COPY)
            for j, t in enumerate(ts):
                nc.vector.tensor_tensor(rep[:, j, :], tables["z", t][:].indirect(u2_sb[:, entries(ci)]), y1[:, j, :], ADD)
            return rep, y2

        def larger(ci, ts, rep, y2):
            top = ring.tile([P, len(ts), CHUNKS[ci]], F32, name="top")
            nc.vector.tensor_tensor(top[:], rep[:], y2[:], MAX)
            return top

        def fetch_and_multiply(ci, ts, top):
            for j, t in enumerate(ts):
                nc.vector.tensor_tensor(
                    hid[ci][:, t, :], tables["zu", t][:].indirect(u1_sb[:, entries(ci)]), top[:, j, :], MULT
                )

        def round_hidden(ci):
            hid_bf = keep.tile([P, CHUNKS[ci], PACK], BF16, name=f"hid_bf{ci}", align_bytes=64)
            rounding_copy = nc.scalar.copy if ci == 0 else nc.vector.tensor_copy
            rounding_copy(
                out=hid_bf[:].rearrange("p (c i) t -> p c t i", i=4),
                in_=hid[ci][:].rearrange("p t (c i) -> p c t i", i=4),
            )
            return hid_bf

        def last_product(ci, hid_bf):
            n = CHUNKS[ci]
            hid_words = keep.tile([P, n], U32, name=f"hid_words{ci}", align_bytes=64)
            hid_scales = keep.tile([P, n], U8, name=f"hid_scales{ci}", align_bytes=64)
            nc.vector.quantize_mx(
                out=hid_words[:].bitcast(FP8X4), scales=hid_scales[:], in_=hid_bf[:].rearrange("p c t -> p (c t)")
            )
            banks = []
            for g0 in range(0, n, GROUP):
                cols = slice(g0, g0 + GROUP)
                acc = psum.tile([P, PACK, GROUP], F32, name="acc")
                for t in range(PACK):
                    nc.tensor.matmul_mx(
                        out=acc[:, t, :], rhs=hid_words[:, cols].bitcast(FP8X4), rhs_scale=hid_scales[:, cols],
                        start=True, stop=True, **stationary(2, 0, t),
                    )
                banks.append((cols, acc))
            return banks

        def store_values(ci, banks):
            n, r0 = CHUNKS[ci], starts[ci]
            res = keep.tile([P, PACK, n], F32, name=f"res{ci}")
            for cols, acc in banks:
                nc.scalar.copy(out=res[:, :, cols], in_=acc[:])
            nc.sync.dma_start(out=out_rows[:, :, r0 : r0 + n], in_=res[:])

        def round_values(ci, banks):
            res_bf = keep.tile([P, CHUNKS[ci], PACK], BF16, name=f"res_bf{ci}", align_bytes=64)
            for cols, acc in banks:
                if ci == final:
                    nc.vector.tensor_copy(out=res_bf[:, cols, :], in_=acc[:].rearrange("p t c -> p c t"))
                else:
                    nc.scalar.copy(out=res_bf[:, cols, :], in_=acc[:].rearrange("p t c -> p c t"))
            return res_bf

        def store_words(ci, res_bf):
            done = slice(starts[ci], starts[ci] + CHUNKS[ci])
            nc.vector.quantize_mx(
                out=out_words[:, done].bitcast(FP8X4), scales=out_scales[:, done],
                in_=res_bf[:].rearrange("p c t -> p (c t)"),
            )
            nc.sync.dma_start(out=out_words_hbm[:, done], in_=out_words[:, done].bitcast(I32))

        waiting_top = None
        waiting_hidden = None
        waiting_values = None
        for ci, ts in steps:
            if ci == 0:
                make_tables(ts[0])
            rep, y2 = fetch_and_add(ci, ts)
            if waiting_hidden is not None:
                banks = last_product(*waiting_hidden)
                store_values(waiting_hidden[0], banks)
                if waiting_values is not None:
                    store_words(*waiting_values)
                waiting_values = (waiting_hidden[0], round_values(waiting_hidden[0], banks))
                waiting_hidden = None
            if waiting_top is not None:
                fetch_and_multiply(*waiting_top)
            top = larger(ci, ts, rep, y2)
            if waiting_top is not None and waiting_top[0] != ci:
                waiting_hidden = (waiting_top[0], round_hidden(waiting_top[0]))
            waiting_top = (ci, ts, top)
        if waiting_hidden is not None:
            banks = last_product(*waiting_hidden)
            store_values(waiting_hidden[0], banks)
            store_words(*waiting_values)
            waiting_values = (waiting_hidden[0], round_values(waiting_hidden[0], banks))
        fetch_and_multiply(*waiting_top)
        banks = last_product(final, round_hidden(final))
        store_words(*waiting_values)
        store_words(final, round_values(final, banks))
        store_values(final, banks)
        for q in range(4):
            queue = nc.scalar if q % 2 else nc.sync
            queue.dma_start(
                out=out_2[0, 4 * q : 4 * q + 4, :].bitcast(I32), in_=out_scales[32 * q : 32 * q + 4, :].bitcast(I32)
            )
